import numpy as np, ml_dtypes
CORES = [8,136,40,168]
N = 4
import mx_ref
NC, KB = 128, 3
BF = ml_dtypes.bfloat16
def cut(t, i, w=512):
    return t[:, w * i:w * i + w]
def term(a, B):
    return np.stack([mx_ref.matmul(mx_ref.quantize(cut(a, i)), B) for i in range(4)], axis=2).reshape(128, -1)
def setup_inputs(rng):
    def f(*shape):
        return mx_ref.flush((rng.standard_normal(shape, dtype=np.float32) * np.exp2(rng.integers(-2, 3, shape[:-1] + (1,)))).astype(BF))
    return {"a": f(N, 128, 4 * 512), "b": f(N, 128, KB * 4 * NC)}
def setup_inputs_blocks(rng):
    d = setup_inputs(rng)
    for k in ("a", "b"): d[k] = mx_ref.spread(d[k], rng, 2)
    return d
def setup_inputs_wide(rng):
    d = setup_inputs(rng)
    for k in ("a", "b"): d[k] = mx_ref.flush((d[k].astype(np.float32) * np.exp2(rng.integers(-4, 5, (N, 1, 1))).astype(np.float32)).astype(BF))
    return d
def setup_inputs_lossless(rng):
    a = np.zeros((N, 128, 4 * 128, 4), np.float32)
    for r in range(N):
        k = rng.integers(0, 512, size=4 * 128)
        a[r, k // 4, np.arange(4 * 128), k % 4] = 1.0
    size = np.repeat(2.0 ** rng.integers(-4, 5, size=(1, 1, (KB * 4 * NC) // 4)), 4, axis=2)
    b = rng.integers(-1, 2, size=(N, 128, KB * 4 * NC)) * size
    return {"a": a.reshape(N, 128, 4 * 512).astype(BF), "b": b.astype(np.float32).astype(BF)}
def reference(a, b):
    y = np.zeros((N, 128, KB * 4 * NC), np.float32)
    for k in range(KB):
        y[:, :, 4 * NC * k:4 * NC * k + 4 * NC] = mx_ref.total([term(a[r], mx_ref.quantize(cut(b[r], k, 4 * NC))) for r in range(N)])
    return {"y": y}

@@ -1,0 +1,156 @@
+from concourse.mybir import dt, AluOpType, ActivationFunctionType
+
+N = 4
+HW = 192
+
+SCRATCH = {
+    "a_t": ("sbuf", [128, 2048], "bfloat16"),
+    "b_t": ("sbuf", [128, 1536], "bfloat16"),
+    "aq": ("sbuf", [128, 512], "float8_e4m3fn_x4"),
+    "asc": ("sbuf", [128, 512], "uint8"),
+    "bq": ("sbuf", [128, 384], "float8_e4m3fn_x4"),
+    "bsc": ("sbuf", [128, 384], "uint8"),
+    "ones": ("sbuf", [128, 128], "bfloat16"),
+    "idn": ("sbuf", [128, 128], "bfloat16"),
+    "e_t": ("sbuf", [128, 2048], "bfloat16"),
+    "eq": ("sbuf", [128, 512], "float8_e4m3fn_x4"),
+    "esc": ("sbuf", [128, 512], "uint8"),
+    "tile": ("sbuf", [128, 1536], "bfloat16"),
+    "tq": ("sbuf", [128, 384], "float8_e4m3fn_x4"),
+    "tsc": ("sbuf", [128, 384], "uint8"),
+    "lq1": ("sbuf", [128, 384], "float8_e4m3fn_x4"),
+    "lq2": ("sbuf", [128, 384], "float8_e4m3fn_x4"),
+    "lq3": ("sbuf", [128, 384], "float8_e4m3fn_x4"),
+    "ls1": ("sbuf", [128, 384], "uint8"),
+    "ls2": ("sbuf", [128, 384], "uint8"),
+    "ls3": ("sbuf", [128, 384], "uint8"),
+    "ps": ("psum", [128, 4096], "float32"),
+    "yst": ("sbuf", [128, 1536], "float32"),
+}
+
+SEMAPHORES = (
+    ["ld_b", "ld_a0", "ld_a1", "ld_a2", "q_b", "q_a0", "q_a1", "q_a2"]
+    + ["pm%d%d" % (i, h) for i in range(4) for h in range(2)]
+    + ["cp0", "cp1", "tqd", "ones_s", "idn_s", "ez_s", "ec_s", "eq_s"]
+    + ["arr1", "arr2", "arr3", "sent"]
+    + ["fin%d%d" % (i, h) for i in range(4) for h in range(2)]
+    + ["oc0", "oc1", "st"]
+)
+
+
+def rank_program(g, core, T, topo):
+    rank = T.rank_of(core)
+    if rank is None:
+        return
+    S = T.sem
+    V, A, PE, SY = g.vector, g.scalar, g.tensor, g.sync
+    COPY = ActivationFunctionType.Copy
+
+    def bank(i, h):
+        k = 2 * i + h
+        return T.ps[:, 512 * k:512 * k + HW]
+
+    def slot(i, h):
+        return i // 2, 2 * (i % 2) + h
+
+    def own(i, h, stop):
+        return PE.matmul_mx(bank(i, h), T.aq[:, 128 * i:128 * i + 128], T.asc[:, 128 * i:128 * i + 128],
+                            T.bq[:, HW * h:HW * h + HW], T.bsc[:, HW * h:HW * h + HW], True, stop)
+
+    SY.dma_start(T.b_t[:], T.b[:]).then_inc(S.ld_b, 16)
+    A.dma_start(T.a_t[:, 0:512], T.a[:, 0:512]).then_inc(S.ld_a0, 16)
+    SY.dma_start(T.a_t[:, 512:1024], T.a[:, 512:1024]).then_inc(S.ld_a1, 16)
+    A.dma_start(T.a_t[:, 1024:2048], T.a[:, 1024:2048]).then_inc(S.ld_a2, 16)
+
+    V.memset(T.ones[:], 1.0).then_inc(S.ones_s, 1)
+    V.memset(T.e_t[:], 0.0).then_inc(S.ez_s, 1)
+    g.wait_ge(S.ones_s, 1)
+    g.affine_select(T.idn[:], T.ones[:], [[-1, 128]], AluOpType.is_equal, 0.0, 0, 1).then_inc(S.idn_s, 1)
+
+    PE.wait_ge(S.q_b, 1)
+    for i in range(4):
+        if i < 3:
+            PE.wait_ge(S["q_a%d" % i], 1)
+        for h in range(2):
+            own(i, h, True).then_inc(S["pm%d%d" % (i, h)], 1)
+
+    def to_tile(eng, i, h):
+        r, t = slot(i, h)
+        eng.wait_ge(S["pm%d%d" % (i, h)], 1)
+        out = T.tile[:, 4 * HW * r + t:4 * HW * (r + 1):4]
+        if eng is V:
+            V.tensor_copy(out, bank(i, h)).then_inc(S["cp%d" % r], 1)
+        else:
+            A.activation(out, bank(i, h), COPY).then_inc(S["cp%d" % r], 1)
+
+    def q_tile(r):
+        V.wait_ge(S["cp%d" % r], 4)
+        V.quantize_mx(T.tq[:, HW * r:HW * (r + 1)], T.tsc[:, HW * r:HW * (r + 1)],
+                      T.tile[:, 4 * HW * r:4 * HW * (r + 1)]).then_inc(S.tqd, 1)
+
+    V.wait_ge(S.ld_b, 16)
+    V.quantize_mx(T.bq[:], T.bsc[:], T.b_t[:]).then_inc(S.q_b, 1)
+    V.wait_ge(S.ld_a0, 16)
+    V.quantize_mx(T.aq[:, 0:128], T.asc[:, 0:128], T.a_t[:, 0:512]).then_inc(S.q_a0, 1)
+    V.wait_ge(S.ld_a1, 16)
+    V.quantize_mx(T.aq[:, 128:256], T.asc[:, 128:256], T.a_t[:, 512:1024]).then_inc(S.q_a1, 1)
+    to_tile(V, 0, 0)
+    V.wait_ge(S.ld_a2, 16)
+    V.quantize_mx(T.aq[:, 256:512], T.asc[:, 256:512], T.a_t[:, 1024:2048]).then_inc(S.q_a2, 1)
+    to_tile(V, 1, 0)
+    q_tile(0)
+    to_tile(V, 2, 0)
+    to_tile(V, 3, 0)
+    q_tile(1)
+    for i in range(4):
+        to_tile(A, i, 1)
+
+    g.wait_ge(S.tqd, 2)
+    sent = 0
+    for d in (1, 2, 3):
+        dst = T.cores[(rank + d) % N]
+        rid, pid = topo.addr(dst, core)
+        m = topo.mask(core, dst)
+        ne = bin(m).count("1")
+        g.remote_dma(T["lq%d" % d][:].bitcast(dt.uint8), T.tq[:].bitcast(dt.uint8), S["arr%d" % d], S.sent, pid, rid, m)
+        g.remote_dma(T["ls%d" % d][:], T.tsc[:], S["arr%d" % d], S.sent, pid, rid, m)
+        sent += 2 * ne
+
+    V.wait_ge(S.ez_s, 1)
+    V.wait_ge(S.idn_s, 1)
+    for t in range(4):
+        V.tensor_copy(T.e_t[:, 512 * t + t:512 * t + 512:4], T.idn[:]).then_inc(S.ec_s, 1)
+    V.wait_ge(S.ec_s, 4)
+    V.quantize_mx(T.eq[:], T.esc[:], T.e_t[:]).then_inc(S.eq_s, 1)
+
+    for r in range(2):
+        PE.wait_ge(S["cp%d" % r], 4)
+        for i in (2 * r, 2 * r + 1):
+            for h in range(2):
+                own(i, h, False)
+    PE.wait_ge(S.eq_s, 1)
+    for d in (1, 2, 3):
+        src = T.cores[(rank - d) % N]
+        PE.wait_ge(S["arr%d" % d], 2 * bin(topo.mask(src, core)).count("1"))
+        for h in range(2):
+            for i in range(4):
+                r, t = slot(i, h)
+                ins = PE.matmul_mx(bank(i, h), T.eq[:, 128 * t:128 * t + 128], T.esc[:, 128 * t:128 * t + 128],
+                                   T["lq%d" % d][:, HW * r:HW * (r + 1)], T["ls%d" % d][:, HW * r:HW * (r + 1)],
+                                   False, d == 3)
+                if d == 3:
+                    ins.then_inc(S["fin%d%d" % (i, h)], 1)
+
+    for h in range(2):
+        for i in range(4):
+            eng = V if i % 2 == 0 else A
+            eng.wait_ge(S["fin%d%d" % (i, h)], 1)
+            out = T.yst[:, 4 * HW * h + i:4 * HW * (h + 1):4]
+            if eng is V:
+                V.tensor_copy(out, bank(i, h)).then_inc(S["oc%d" % h], 1)
+            else:
+                A.activation(out, bank(i, h), COPY).then_inc(S["oc%d" % h], 1)
+        SY.wait_ge(S["oc%d" % h], 4)
+        SY.dma_start(T.y[:, 4 * HW * h:4 * HW * (h + 1)], T.yst[:, 4 * HW * h:4 * HW * (h + 1)]).then_inc(S.st, 16)
+    SY.wait_ge(S.st, 32)
+    g.wait_ge(S.sent, sent)

@@ -1,3 +1,4 @@
+from concourse.bass import DstId, RemoteDMATransfer
 from concourse.mybir import dt, AluOpType, ActivationFunctionType
 
 N = 4
@@ -29,10 +30,10 @@ SCRATCH = {
 }
 
 SEMAPHORES = (
-    ["ld_b", "ld_a0", "ld_a1", "ld_a2", "q_b", "q_a0", "q_a1", "q_a2"]
+    ["ld_b0", "ld_b1", "ld_a0", "ld_a1", "q_b0", "q_b1", "q_a0", "q_a1"]
     + ["pm%d%d" % (i, h) for i in range(4) for h in range(2)]
-    + ["cp0", "cp1", "tqd", "ones_s", "idn_s", "ez_s", "ec_s", "eq_s"]
-    + ["arr1", "arr2", "arr3", "sent"]
+    + ["cp0", "cp1", "tq0", "tq1", "ones_s", "idn_s", "ez_s", "ec_s", "eq_s"]
+    + ["early", "sc1", "sc2", "sc3", "cd1", "cd2", "cd3", "sent"]
     + ["fin%d%d" % (i, h) for i in range(4) for h in range(2)]
     + ["oc0", "oc1", "st"]
 )
@@ -45,75 +46,94 @@ def rank_program(g, core, T, topo):
     S = T.sem
     V, A, PE, SY = g.vector, g.scalar, g.tensor, g.sync
     COPY = ActivationFunctionType.Copy
+    W4 = 4 * HW
+
+    def engines(src, dst):
+        return bin(topo.mask(src, dst)).count("1")
 
     def bank(i, h):
-        k = 2 * i + h
+        k = 4 * h + i
         return T.ps[:, 512 * k:512 * k + HW]
-
-    def slot(i, h):
-        return i // 2, 2 * (i % 2) + h
 
     def own(i, h, stop):
         return PE.matmul_mx(bank(i, h), T.aq[:, 128 * i:128 * i + 128], T.asc[:, 128 * i:128 * i + 128],
                             T.bq[:, HW * h:HW * h + HW], T.bsc[:, HW * h:HW * h + HW], True, stop)
 
-    SY.dma_start(T.b_t[:], T.b[:]).then_inc(S.ld_b, 16)
-    A.dma_start(T.a_t[:, 0:512], T.a[:, 0:512]).then_inc(S.ld_a0, 16)
-    SY.dma_start(T.a_t[:, 512:1024], T.a[:, 512:1024]).then_inc(S.ld_a1, 16)
-    A.dma_start(T.a_t[:, 1024:2048], T.a[:, 1024:2048]).then_inc(S.ld_a2, 16)
+    SY.dma_start(T.b_t[:, 0:W4], T.b[:, 0:W4]).then_inc(S.ld_b0, 16)
+    A.dma_start(T.a_t[:, 0:1024], T.a[:, 0:1024]).then_inc(S.ld_a0, 16)
+    SY.dma_start(T.a_t[:, 1024:2048], T.a[:, 1024:2048]).then_inc(S.ld_a1, 16)
+    A.dma_start(T.b_t[:, W4:2 * W4], T.b[:, W4:2 * W4]).then_inc(S.ld_b1, 16)
 
     V.memset(T.ones[:], 1.0).then_inc(S.ones_s, 1)
     V.memset(T.e_t[:], 0.0).then_inc(S.ez_s, 1)
     g.wait_ge(S.ones_s, 1)
     g.affine_select(T.idn[:], T.ones[:], [[-1, 128]], AluOpType.is_equal, 0.0, 0, 1).then_inc(S.idn_s, 1)
 
-    PE.wait_ge(S.q_b, 1)
-    for i in range(4):
-        if i < 3:
-            PE.wait_ge(S["q_a%d" % i], 1)
-        for h in range(2):
+    for h in range(2):
+        PE.wait_ge(S["q_b%d" % h], 1)
+        for i in range(4):
+            if h == 0 and i % 2 == 0:
+                PE.wait_ge(S["q_a%d" % (i // 2)], 1)
             own(i, h, True).then_inc(S["pm%d%d" % (i, h)], 1)
 
     def to_tile(eng, i, h):
-        r, t = slot(i, h)
         eng.wait_ge(S["pm%d%d" % (i, h)], 1)
-        out = T.tile[:, 4 * HW * r + t:4 * HW * (r + 1):4]
+        out = T.tile[:, W4 * h + i:W4 * (h + 1):4]
         if eng is V:
-            V.tensor_copy(out, bank(i, h)).then_inc(S["cp%d" % r], 1)
+            V.tensor_copy(out, bank(i, h)).then_inc(S["cp%d" % h], 1)
         else:
-            A.activation(out, bank(i, h), COPY).then_inc(S["cp%d" % r], 1)
+            A.activation(out, bank(i, h), COPY).then_inc(S["cp%d" % h], 1)
 
-    def q_tile(r):
-        V.wait_ge(S["cp%d" % r], 4)
-        V.quantize_mx(T.tq[:, HW * r:HW * (r + 1)], T.tsc[:, HW * r:HW * (r + 1)],
-                      T.tile[:, 4 * HW * r:4 * HW * (r + 1)]).then_inc(S.tqd, 1)
+    def q_in(h, name):
+        V.wait_ge(S["ld_%s%d" % (name, h)], 16)
+        if name == "b":
+            V.quantize_mx(T.bq[:, HW * h:HW * (h + 1)], T.bsc[:, HW * h:HW * (h + 1)],
+                          T.b_t[:, W4 * h:W4 * (h + 1)]).then_inc(S["q_b%d" % h], 1)
+        else:
+            V.quantize_mx(T.aq[:, 256 * h:256 * (h + 1)], T.asc[:, 256 * h:256 * (h + 1)],
+                          T.a_t[:, 1024 * h:1024 * (h + 1)]).then_inc(S["q_a%d" % h], 1)
 
-    V.wait_ge(S.ld_b, 16)
-    V.quantize_mx(T.bq[:], T.bsc[:], T.b_t[:]).then_inc(S.q_b, 1)
-    V.wait_ge(S.ld_a0, 16)
-    V.quantize_mx(T.aq[:, 0:128], T.asc[:, 0:128], T.a_t[:, 0:512]).then_inc(S.q_a0, 1)
-    V.wait_ge(S.ld_a1, 16)
-    V.quantize_mx(T.aq[:, 128:256], T.asc[:, 128:256], T.a_t[:, 512:1024]).then_inc(S.q_a1, 1)
+    def q_tile(h):
+        V.wait_ge(S["cp%d" % h], 4)
+        V.quantize_mx(T.tq[:, HW * h:HW * (h + 1)], T.tsc[:, HW * h:HW * (h + 1)],
+                      T.tile[:, W4 * h:W4 * (h + 1)]).then_inc(S["tq%d" % h], 1)
+
+    q_in(0, "b")
+    q_in(0, "a")
     to_tile(V, 0, 0)
-    V.wait_ge(S.ld_a2, 16)
-    V.quantize_mx(T.aq[:, 256:512], T.asc[:, 256:512], T.a_t[:, 1024:2048]).then_inc(S.q_a2, 1)
-    to_tile(V, 1, 0)
+    q_in(1, "a")
+    q_in(1, "b")
     q_tile(0)
-    to_tile(V, 2, 0)
-    to_tile(V, 3, 0)
+    to_tile(V, 0, 1)
+    to_tile(V, 2, 1)
     q_tile(1)
-    for i in range(4):
+    for i in (1, 2, 3):
+        to_tile(A, i, 0)
+    for i in (1, 3):
         to_tile(A, i, 1)
 
-    g.wait_ge(S.tqd, 2)
+    dsts = [T.cores[(rank + d) % N] for d in (1, 2, 3)]
+    m = topo.mask(core, dsts[0])
+    for dst in dsts:
+        m &= topo.mask(core, dst)
+    ne = bin(m).count("1")
     sent = 0
-    for d in (1, 2, 3):
-        dst = T.cores[(rank + d) % N]
+    g.wait_ge(S.tq0, 1)
+    ids = []
+    for dst in dsts:
         rid, pid = topo.addr(dst, core)
-        m = topo.mask(core, dst)
-        ne = bin(m).count("1")
-        g.remote_dma(T["lq%d" % d][:].bitcast(dt.uint8), T.tq[:].bitcast(dt.uint8), S["arr%d" % d], S.sent, pid, rid, m)
-        g.remote_dma(T["ls%d" % d][:], T.tsc[:], S["arr%d" % d], S.sent, pid, rid, m)
+        ids.append(DstId(rid=rid, pnc=pid))
+    g.remote_dma_fused([RemoteDMATransfer(dst_ids=ids, dma_engine_mask=m, remote_sem=S.early,
+                                          srcs=[T.tq[:, 0:HW].bitcast(dt.uint8)],
+                                          dsts=[T["lq%d" % d][:, 0:HW].bitcast(dt.uint8) for d in (1, 2, 3)])],
+                       local_sem=S.sent)
+    sent += ne
+    g.wait_ge(S.tq1, 1)
+    for d in (1, 2, 3):
+        rid, pid = topo.addr(dsts[d - 1], core)
+        g.remote_dma(T["ls%d" % d][:], T.tsc[:], S["sc%d" % d], S.sent, pid, rid, m)
+        g.remote_dma(T["lq%d" % d][:, HW:2 * HW].bitcast(dt.uint8), T.tq[:, HW:2 * HW].bitcast(dt.uint8),
+                     S["cd%d" % d], S.sent, pid, rid, m)
         sent += 2 * ne
 
     V.wait_ge(S.ez_s, 1)
@@ -123,20 +143,18 @@ def rank_program(g, core, T, topo):
     V.wait_ge(S.ec_s, 4)
     V.quantize_mx(T.eq[:], T.esc[:], T.e_t[:]).then_inc(S.eq_s, 1)
 
-    for r in range(2):
-        PE.wait_ge(S["cp%d" % r], 4)
-        for i in (2 * r, 2 * r + 1):
-            for h in range(2):
-                own(i, h, False)
+    for h in range(2):
+        PE.wait_ge(S["cp%d" % h], 4)
+        for i in range(4):
+            own(i, h, False)
     PE.wait_ge(S.eq_s, 1)
+    PE.wait_ge(S.early, 3 * ne)
     for d in (1, 2, 3):
-        src = T.cores[(rank - d) % N]
-        PE.wait_ge(S["arr%d" % d], 2 * bin(topo.mask(src, core)).count("1"))
         for h in range(2):
+            PE.wait_ge(S[("sc%d" if h == 0 else "cd%d") % d], ne)
             for i in range(4):
-                r, t = slot(i, h)
-                ins = PE.matmul_mx(bank(i, h), T.eq[:, 128 * t:128 * t + 128], T.esc[:, 128 * t:128 * t + 128],
-                                   T["lq%d" % d][:, HW * r:HW * (r + 1)], T["ls%d" % d][:, HW * r:HW * (r + 1)],
+                ins = PE.matmul_mx(bank(i, h), T.eq[:, 128 * i:128 * i + 128], T.esc[:, 128 * i:128 * i + 128],
+                                   T["lq%d" % d][:, HW * h:HW * (h + 1)], T["ls%d" % d][:, HW * h:HW * (h + 1)],
                                    False, d == 3)
                 if d == 3:
                     ins.then_inc(S["fin%d%d" % (i, h)], 1)
@@ -145,12 +163,12 @@ def rank_program(g, core, T, topo):
         for i in range(4):
             eng = V if i % 2 == 0 else A
             eng.wait_ge(S["fin%d%d" % (i, h)], 1)
-            out = T.yst[:, 4 * HW * h + i:4 * HW * (h + 1):4]
+            out = T.yst[:, W4 * h + i:W4 * (h + 1):4]
             if eng is V:
                 V.tensor_copy(out, bank(i, h)).then_inc(S["oc%d" % h], 1)
             else:
                 A.activation(out, bank(i, h), COPY).then_inc(S["oc%d" % h], 1)
         SY.wait_ge(S["oc%d" % h], 4)
-        SY.dma_start(T.y[:, 4 * HW * h:4 * HW * (h + 1)], T.yst[:, 4 * HW * h:4 * HW * (h + 1)]).then_inc(S.st, 16)
+        SY.dma_start(T.y[:, W4 * h:W4 * (h + 1)], T.yst[:, W4 * h:W4 * (h + 1)]).then_inc(S.st, 16)
     SY.wait_ge(S.st, 32)
     g.wait_ge(S.sent, sent)

@@ -3,6 +3,7 @@ from concourse.mybir import dt, AluOpType, ActivationFunctionType
 
 N = 4
 HW = 192
+WORLD = 256
 
 SCRATCH = {
     "a_t": ("sbuf", [128, 2048], "bfloat16"),
@@ -19,6 +20,7 @@ SCRATCH = {
     "tile": ("sbuf", [128, 1536], "bfloat16"),
     "tq": ("sbuf", [128, 384], "float8_e4m3fn_x4"),
     "tsc": ("sbuf", [128, 384], "uint8"),
+    "hq": ("sbuf", [128, HW], "float8_e4m3fn_x4"),
     "lq1": ("sbuf", [128, 384], "float8_e4m3fn_x4"),
     "lq2": ("sbuf", [128, 384], "float8_e4m3fn_x4"),
     "lq3": ("sbuf", [128, 384], "float8_e4m3fn_x4"),
@@ -33,23 +35,45 @@ SEMAPHORES = (
     ["ld_b0", "ld_b1", "ld_a0", "ld_a1", "q_b0", "q_b1", "q_a0", "q_a1"]
     + ["pm%d%d" % (i, h) for i in range(4) for h in range(2)]
     + ["cp0", "cp1", "tq0", "tq1", "ones_s", "idn_s", "ez_s", "ec_s", "eq_s"]
-    + ["early", "sc1", "sc2", "sc3", "cd1", "cd2", "cd3", "sent"]
+    + ["hin", "ea1", "ea2", "ea3", "sc1", "sc2", "sc3", "cd1", "cd2", "cd3", "sent"]
     + ["fin%d%d" % (i, h) for i in range(4) for h in range(2)]
     + ["oc0", "oc1", "st"]
 )
 
 
+def count(mask):
+    return bin(mask).count("1")
+
+
+def helper_of(c, cores, topo):
+    for w in range(WORLD):
+        if (topo.host(w) == topo.host(c) and topo.chip(w) == topo.chip(c) and topo.die(w) != topo.die(c)
+                and all(topo.may_write(w, o) for o in cores if o != c)):
+            return w
+    return None
+
+
 def rank_program(g, core, T, topo):
+    S = T.sem
     rank = T.rank_of(core)
     if rank is None:
+        for r in range(N):
+            if helper_of(T.cores[r], T.cores, topo) == core:
+                src = T.cores[r]
+                g.wait_ge(S.hin, count(topo.mask(src, core) & ~topo.mask(src, T.cores[(r + 1) % N])))
+                out = 0
+                for d in (2, 3):
+                    dst = T.cores[(r + d) % N]
+                    rid, pid = topo.addr(dst, core)
+                    hm = topo.mask(core, dst)
+                    g.remote_dma(T["lq%d" % d][:, 0:HW].bitcast(dt.uint8), T.hq[:].bitcast(dt.uint8),
+                                 S["ea%d" % d], S.sent, pid, rid, hm)
+                    out += count(hm)
+                g.wait_ge(S.sent, out)
         return
-    S = T.sem
     V, A, PE, SY = g.vector, g.scalar, g.tensor, g.sync
     COPY = ActivationFunctionType.Copy
     W4 = 4 * HW
-
-    def engines(src, dst):
-        return bin(topo.mask(src, dst)).count("1")
 
     def bank(i, h):
         k = 4 * h + i
@@ -116,17 +140,16 @@ def rank_program(g, core, T, topo):
     m = topo.mask(core, dsts[0])
     for dst in dsts:
         m &= topo.mask(core, dst)
-    ne = bin(m).count("1")
+    ne = count(m)
+    helper = helper_of(core, T.cores, topo)
+    m_on = topo.mask(core, helper) & ~topo.mask(core, dsts[0])
     sent = 0
     g.wait_ge(S.tq0, 1)
-    ids = []
-    for dst in dsts:
-        rid, pid = topo.addr(dst, core)
-        ids.append(DstId(rid=rid, pnc=pid))
-    g.remote_dma_fused([RemoteDMATransfer(dst_ids=ids, dma_engine_mask=m, remote_sem=S.early,
-                                          srcs=[T.tq[:, 0:HW].bitcast(dt.uint8)],
-                                          dsts=[T["lq%d" % d][:, 0:HW].bitcast(dt.uint8) for d in (1, 2, 3)])],
-                       local_sem=S.sent)
+    rid, pid = topo.addr(helper, core)
+    g.remote_dma(T.hq[:].bitcast(dt.uint8), T.tq[:, 0:HW].bitcast(dt.uint8), S.hin, S.sent, pid, rid, m_on)
+    sent += count(m_on)
+    rid, pid = topo.addr(dsts[0], core)
+    g.remote_dma(T.lq1[:, 0:HW].bitcast(dt.uint8), T.tq[:, 0:HW].bitcast(dt.uint8), S.ea1, S.sent, pid, rid, m)
     sent += ne
     g.wait_ge(S.tq1, 1)
     for d in (1, 2, 3):
@@ -148,10 +171,13 @@ def rank_program(g, core, T, topo):
         for i in range(4):
             own(i, h, False)
     PE.wait_ge(S.eq_s, 1)
-    PE.wait_ge(S.early, 3 * ne)
     for d in (1, 2, 3):
+        sender = T.cores[(rank - d) % N]
+        via = sender if d == 1 else helper_of(sender, T.cores, topo)
         for h in range(2):
             PE.wait_ge(S[("sc%d" if h == 0 else "cd%d") % d], ne)
+            if h == 0:
+                PE.wait_ge(S["ea%d" % d], count(topo.mask(via, core)))
             for i in range(4):
                 ins = PE.matmul_mx(bank(i, h), T.eq[:, 128 * i:128 * i + 128], T.esc[:, 128 * i:128 * i + 128],
                                    T["lq%d" % d][:, HW * h:HW * (h + 1)], T["ls%d" % d][:, HW * h:HW * (h + 1)],

from concourse.bass import DstId, RemoteDMATransfer
from concourse.mybir import dt, AluOpType, ActivationFunctionType

N = 4
HW = 192
WORLD = 256

SCRATCH = {
    "a_t": ("sbuf", [128, 2048], "bfloat16"),
    "b_t": ("sbuf", [128, 1536], "bfloat16"),
    "aq": ("sbuf", [128, 512], "float8_e4m3fn_x4"),
    "asc": ("sbuf", [128, 512], "uint8"),
    "bq": ("sbuf", [128, 384], "float8_e4m3fn_x4"),
    "bsc": ("sbuf", [128, 384], "uint8"),
    "ones": ("sbuf", [128, 128], "bfloat16"),
    "idn": ("sbuf", [128, 128], "bfloat16"),
    "e_t": ("sbuf", [128, 2048], "bfloat16"),
    "eq": ("sbuf", [128, 512], "float8_e4m3fn_x4"),
    "esc": ("sbuf", [128, 512], "uint8"),
    "tile": ("sbuf", [128, 1536], "bfloat16"),
    "tq": ("sbuf", [128, 384], "float8_e4m3fn_x4"),
    "tsc": ("sbuf", [128, 384], "uint8"),
    "hq": ("sbuf", [128, HW], "float8_e4m3fn_x4"),
    "lq1": ("sbuf", [128, 384], "float8_e4m3fn_x4"),
    "lq2": ("sbuf", [128, 384], "float8_e4m3fn_x4"),
    "lq3": ("sbuf", [128, 384], "float8_e4m3fn_x4"),
    "ls1": ("sbuf", [128, 384], "uint8"),
    "ls2": ("sbuf", [128, 384], "uint8"),
    "ls3": ("sbuf", [128, 384], "uint8"),
    "ps": ("psum", [128, 4096], "float32"),
    "yst": ("sbuf", [128, 1536], "float32"),
}

SEMAPHORES = (
    ["ld_b0", "ld_b1", "ld_a0", "ld_a1", "q_b0", "q_b1", "q_a0", "q_a1"]
    + ["pm%d%d" % (i, h) for i in range(4) for h in range(2)]
    + ["cp0", "cp1", "tq0", "tq1", "ones_s", "idn_s", "ez_s", "ec_s", "eq_s"]
    + ["hin", "ea1", "ea2", "ea3", "sc1", "sc2", "sc3", "cd1", "cd2", "cd3", "sent"]
    + ["fin%d%d" % (i, h) for i in range(4) for h in range(2)]
    + ["oc0", "oc1", "st"]
)


def count(mask):
    return bin(mask).count("1")


def helper_of(c, cores, topo):
    for w in range(WORLD):
        if (topo.host(w) == topo.host(c) and topo.chip(w) == topo.chip(c) and topo.die(w) != topo.die(c)
                and all(topo.may_write(w, o) for o in cores if o != c)):
            return w
    return None


def rank_program(g, core, T, topo):
    S = T.sem
    rank = T.rank_of(core)
    if rank is None:
        for r in range(N):
            if helper_of(T.cores[r], T.cores, topo) == core:
                src = T.cores[r]
                g.wait_ge(S.hin, count(topo.mask(src, core) & ~topo.mask(src, T.cores[(r + 1) % N])))
                out = 0
                for d in (2, 3):
                    dst = T.cores[(r + d) % N]
                    rid, pid = topo.addr(dst, core)
                    hm = topo.mask(core, dst)
                    g.remote_dma(T["lq%d" % d][:, 0:HW].bitcast(dt.uint8), T.hq[:].bitcast(dt.uint8),
                                 S["ea%d" % d], S.sent, pid, rid, hm)
                    out += count(hm)
                g.wait_ge(S.sent, out)
        return
    V, A, PE, SY = g.vector, g.scalar, g.tensor, g.sync
    COPY = ActivationFunctionType.Copy
    W4 = 4 * HW

    def bank(i, h):
        k = 4 * h + i
        return T.ps[:, 512 * k:512 * k + HW]

    def own(i, h, stop):
        return PE.matmul_mx(bank(i, h), T.aq[:, 128 * i:128 * i + 128], T.asc[:, 128 * i:128 * i + 128],
                            T.bq[:, HW * h:HW * h + HW], T.bsc[:, HW * h:HW * h + HW], True, stop)

    SY.dma_start(T.b_t[:, 0:W4], T.b[:, 0:W4]).then_inc(S.ld_b0, 16)
    A.dma_start(T.a_t[:, 0:1024], T.a[:, 0:1024]).then_inc(S.ld_a0, 16)
    SY.dma_start(T.a_t[:, 1024:2048], T.a[:, 1024:2048]).then_inc(S.ld_a1, 16)
    A.dma_start(T.b_t[:, W4:2 * W4], T.b[:, W4:2 * W4]).then_inc(S.ld_b1, 16)

    V.memset(T.ones[:], 1.0).then_inc(S.ones_s, 1)
    V.memset(T.e_t[:], 0.0).then_inc(S.ez_s, 1)
    g.wait_ge(S.ones_s, 1)
    g.affine_select(T.idn[:], T.ones[:], [[-1, 128]], AluOpType.is_equal, 0.0, 0, 1).then_inc(S.idn_s, 1)

    for h in range(2):
        PE.wait_ge(S["q_b%d" % h], 1)
        for i in range(4):
            if h == 0 and i % 2 == 0:
                PE.wait_ge(S["q_a%d" % (i // 2)], 1)
            own(i, h, True).then_inc(S["pm%d%d" % (i, h)], 1)

    def to_tile(eng, i, h):
        eng.wait_ge(S["pm%d%d" % (i, h)], 1)
        out = T.tile[:, W4 * h + i:W4 * (h + 1):4]
        if eng is V:
            V.tensor_copy(out, bank(i, h)).then_inc(S["cp%d" % h], 1)
        else:
            A.activation(out, bank(i, h), COPY).then_inc(S["cp%d" % h], 1)

    def q_in(h, name):
        V.wait_ge(S["ld_%s%d" % (name, h)], 16)
        if name == "b":
            V.quantize_mx(T.bq[:, HW * h:HW * (h + 1)], T.bsc[:, HW * h:HW * (h + 1)],
                          T.b_t[:, W4 * h:W4 * (h + 1)]).then_inc(S["q_b%d" % h], 1)
        else:
            V.quantize_mx(T.aq[:, 256 * h:256 * (h + 1)], T.asc[:, 256 * h:256 * (h + 1)],
                          T.a_t[:, 1024 * h:1024 * (h + 1)]).then_inc(S["q_a%d" % h], 1)

    def q_tile(h):
        V.wait_ge(S["cp%d" % h], 4)
        V.quantize_mx(T.tq[:, HW * h:HW * (h + 1)], T.tsc[:, HW * h:HW * (h + 1)],
                      T.tile[:, W4 * h:W4 * (h + 1)]).then_inc(S["tq%d" % h], 1)

    q_in(0, "b")
    q_in(0, "a")
    to_tile(V, 0, 0)
    q_in(1, "a")
    q_in(1, "b")
    q_tile(0)
    to_tile(V, 0, 1)
    to_tile(V, 2, 1)
    q_tile(1)
    for i in (1, 2, 3):
        to_tile(A, i, 0)
    for i in (1, 3):
        to_tile(A, i, 1)

    dsts = [T.cores[(rank + d) % N] for d in (1, 2, 3)]
    m = topo.mask(core, dsts[0])
    for dst in dsts:
        m &= topo.mask(core, dst)
    ne = count(m)
    helper = helper_of(core, T.cores, topo)
    m_on = topo.mask(core, helper) & ~topo.mask(core, dsts[0])
    sent = 0
    g.wait_ge(S.tq0, 1)
    rid, pid = topo.addr(helper, core)
    g.remote_dma(T.hq[:].bitcast(dt.uint8), T.tq[:, 0:HW].bitcast(dt.uint8), S.hin, S.sent, pid, rid, m_on)
    sent += count(m_on)
    rid, pid = topo.addr(dsts[0], core)
    g.remote_dma(T.lq1[:, 0:HW].bitcast(dt.uint8), T.tq[:, 0:HW].bitcast(dt.uint8), S.ea1, S.sent, pid, rid, m)
    sent += ne
    g.wait_ge(S.tq1, 1)
    for d in (1, 2, 3):
        rid, pid = topo.addr(dsts[d - 1], core)
        g.remote_dma(T["ls%d" % d][:], T.tsc[:], S["sc%d" % d], S.sent, pid, rid, m)
        g.remote_dma(T["lq%d" % d][:, HW:2 * HW].bitcast(dt.uint8), T.tq[:, HW:2 * HW].bitcast(dt.uint8),
                     S["cd%d" % d], S.sent, pid, rid, m)
        sent += 2 * ne

    V.wait_ge(S.ez_s, 1)
    V.wait_ge(S.idn_s, 1)
    for t in range(4):
        V.tensor_copy(T.e_t[:, 512 * t + t:512 * t + 512:4], T.idn[:]).then_inc(S.ec_s, 1)
    V.wait_ge(S.ec_s, 4)
    V.quantize_mx(T.eq[:], T.esc[:], T.e_t[:]).then_inc(S.eq_s, 1)

    for h in range(2):
        PE.wait_ge(S["cp%d" % h], 4)
        for i in range(4):
            own(i, h, False)
    PE.wait_ge(S.eq_s, 1)
    for d in (1, 2, 3):
        sender = T.cores[(rank - d) % N]
        via = sender if d == 1 else helper_of(sender, T.cores, topo)
        for h in range(2):
            PE.wait_ge(S[("sc%d" if h == 0 else "cd%d") % d], ne)
            if h == 0:
                PE.wait_ge(S["ea%d" % d], count(topo.mask(via, core)))
            for i in range(4):
                ins = PE.matmul_mx(bank(i, h), T.eq[:, 128 * i:128 * i + 128], T.esc[:, 128 * i:128 * i + 128],
                                   T["lq%d" % d][:, HW * h:HW * (h + 1)], T["ls%d" % d][:, HW * h:HW * (h + 1)],
                                   False, d == 3)
                if d == 3:
                    ins.then_inc(S["fin%d%d" % (i, h)], 1)

    for h in range(2):
        for i in range(4):
            eng = V if i % 2 == 0 else A
            eng.wait_ge(S["fin%d%d" % (i, h)], 1)
            out = T.yst[:, W4 * h + i:W4 * (h + 1):4]
            if eng is V:
                V.tensor_copy(out, bank(i, h)).then_inc(S["oc%d" % h], 1)
            else:
                A.activation(out, bank(i, h), COPY).then_inc(S["oc%d" % h], 1)
        SY.wait_ge(S["oc%d" % h], 4)
        SY.dma_start(T.y[:, W4 * h:W4 * (h + 1)], T.yst[:, W4 * h:W4 * (h + 1)]).then_inc(S.st, 16)
    SY.wait_ge(S.st, 32)
    g.wait_ge(S.sent, sent)
